import numpy as np
import ml_dtypes


def mxq(x, axis, fmt="e4m3"):
    dtype, down = {"e4m3": (ml_dtypes.float8_e4m3fn, 7), "e5m2": (ml_dtypes.float8_e5m2, 14)}[fmt]
    v = np.moveaxis(np.asarray(x, np.float32).astype(ml_dtypes.bfloat16).astype(np.float64), axis, -1)
    blocks = v.reshape(v.shape[:-1] + (-1, 32))
    amax = np.abs(blocks).max(-1, keepdims=True)
    byte = np.maximum(np.where(amax > 0, np.frexp(amax)[1] - 1 + 127, 0) - down, 1)
    scale = np.exp2(byte - 127.0)
    codes = (blocks / scale).astype(np.float32).astype(dtype).astype(np.float64)
    return np.moveaxis((codes * scale).reshape(v.shape), -1, axis)


WIDE = False


def mx_kscale(k):
    if not WIDE:
        return np.ones(k)
    levels = np.array([10, -10, 5, -5, 0])
    if k % 512:
        return np.exp2(np.random.permutation(np.resize(levels, k // 32))).repeat(32)
    a = np.empty((k // 512, 16))
    for p in range(k // 512):
        a[p, :8] = np.random.permutation(np.resize(levels, 8))
        for g in range(8):
            far = levels[np.abs(levels - a[p, g]) >= 10]
            a[p, g + 8] = far[np.random.randint(len(far))]
    return np.exp2(a.ravel()).repeat(32)


def f64(x):
    return np.asarray(x).astype(np.float64)


def striped(idx):
    return np.tile(idx.reshape(-1, 16).T, (8, 1)).astype(np.uint16)


def unstriped(offs):
    return offs[:16].T.reshape(-1).astype(np.int64)


def pack_weight(w):
    k, n = w.shape
    w = f64(np.asarray(w, np.float32).astype(ml_dtypes.bfloat16)).reshape(k // 32, 32, n)
    amax = np.abs(w).max(1)
    byte = np.clip(np.where(amax > 0, np.frexp(amax)[1] - 1 + 127 - 7, 1), 1, 254)
    scaled = (w * np.exp2(127.0 - byte)[:, None, :]).reshape(k, n).astype(np.float32)
    words = np.ascontiguousarray(scaled.reshape(k // 512, 128, 4, n).transpose(0, 1, 3, 2)).astype(ml_dtypes.float8_e4m3fn).view(np.uint8)
    return words, np.ascontiguousarray(byte.astype(np.uint8).reshape(k // 512, 16, n))


def unpack_weight(words, scales):
    g, p, n, _ = words.shape
    vals = np.ascontiguousarray(words).view(ml_dtypes.float8_e4m3fn).astype(np.float64) * np.repeat(np.exp2(scales.astype(np.float64) - 127.0), 8, axis=1)[..., None]
    return vals.transpose(0, 1, 3, 2).reshape(g * 512, n)


def gelu(v):
    return 0.5 * v * (1.0 + np.tanh(np.sqrt(2.0 / np.pi) * (v + 0.044715 * v**3)))


K, T, S, V, N = 512, 4096, 1024, 512, 128
P = 2 ** 7


def setup_inputs():
    n = np.random.standard_normal
    s = mx_kscale(K)[:, None]
    packed_xT = pack_weight(n((K, T)) * s)
    return {
        "x_words": packed_xT[0],
        "x_scales": packed_xT[1],
        "w1": (n((K, N)) / np.sqrt(K) / s).astype(np.float32),
        "frac": np.tile(np.random.uniform(0.05, 0.95, V), (P, 1)).astype(np.float32),
        "offs": striped(np.random.permutation(T)[:S]),
        "left": striped(np.random.permutation(S)[:V]),
        "right": striped(np.random.permutation(S)[:V]),
    }


def reference(x_words, x_scales, w1, frac, offs, left, right):
    xq = unpack_weight(x_words, x_scales)[:, unstriped(offs)]
    y = gelu(mxq(f64(w1), 0, "e4m3").T @ xq)
    l = y[:, unstriped(left)]
    return l + (y[:, unstriped(right)] - l) * f64(frac)[:1]

@@ -1,0 +1,110 @@
+from contextlib import ExitStack
+
+import concourse.mybir as mybir
+
+K, T, S, V, M = 512, 4096, 1024, 512, 128
+FLOPS = 2 * K * M * S
+
+F32 = mybir.dt.float32
+BF16 = mybir.dt.bfloat16
+I32 = mybir.dt.int32
+U32 = mybir.dt.uint32
+U16 = mybir.dt.uint16
+U8 = mybir.dt.uint8
+FP8X4 = mybir.dt.float8_e4m3fn_x4
+MULT = mybir.AluOpType.mult
+ADD = mybir.AluOpType.add
+GELU = mybir.ActivationFunctionType.Gelu_apprx_tanh
+
+P = 128
+PACK = 4
+LIST_ROWS = 16
+HALF = S // 2
+PIECES = ((512,), (128, 128, 128, 128))
+OUT_PIECE = V // 2
+
+
+def tile_picked_lerp_gelu_p_kernel(tc, x_words, x_scales, w1, frac, offs, left, right, out):
+    nc = tc.nc
+    with ExitStack() as ctx:
+        keep = ctx.enter_context(tc.tile_pool(name="keep", bufs=1))
+        shared = ctx.enter_context(tc.tile_pool(name="shared", bufs=1))
+        psum = ctx.enter_context(tc.psum_pool(name="psum", bufs=1))
+
+        offs_sb = keep.tile([P, S // LIST_ROWS], U16, name="offs_sb")
+        left_sb = keep.tile([P, V // LIST_ROWS], U16, name="left_sb")
+        right_sb = keep.tile([P, V // LIST_ROWS], U16, name="right_sb")
+        words = keep.tile([P, T], I32, name="words", align_bytes=64)
+        spread = shared.tile([P, T], U8, name="spread", align_bytes=64, offset=0)
+        w_raw = keep.tile([P, PACK, M], F32, name="w_raw", align_bytes=64)
+        frac_sb = keep.tile([P, V], F32, name="frac_sb", align_bytes=64)
+        x_plane = keep.tile([P, S], U8, name="x_plane", align_bytes=64)
+
+        words_hbm = x_words[0].rearrange("p n t -> p (n t)").bitcast(I32)
+        for h in range(2):
+            cols = slice(h * T // 2, (h + 1) * T // 2)
+            nc.scalar.dma_start(out=words[:, cols], in_=words_hbm[:, cols])
+        nc.scalar.dma_start(out=frac_sb[:], in_=frac)
+
+        nc.vector.memset(spread[:].bitcast(I32), 0)
+        nc.gpsimd.memset(x_plane[:].bitcast(I32), 0)
+        nc.sync.dma_start(offs_sb[:], offs)
+        nc.sync.dma_start(out=spread[4:P:8, :].bitcast(I32), in_=x_scales[0].bitcast(I32))
+        nc.sync.dma_start(out=w_raw[:], in_=w1.rearrange("(p j) m -> p j m", j=PACK))
+        nc.sync.dma_start(left_sb[:], left)
+        nc.sync.dma_start(right_sb[:], right)
+
+        picked_spread = keep.tile([P, S], U8, name="picked_spread", align_bytes=64)
+        nc.vector.tensor_copy(picked_spread[:], spread[:].indirect(offs_sb[:]))
+        for q in range(4):
+            nc.sync.dma_start(
+                out=x_plane[32 * q : 32 * q + 4, :].bitcast(I32),
+                in_=picked_spread[32 * q + 4 : 32 * q + 32 : 8, :].bitcast(I32),
+            )
+
+        w_bf = shared.tile([P, M, PACK], BF16, name="w_bf", align_bytes=64, offset=T)
+        w_codes = keep.tile([P, M], U32, name="w_codes", align_bytes=64)
+        w_plane = keep.tile([P, M], U8, name="w_plane", align_bytes=64)
+        nc.vector.tensor_copy(out=w_bf[:], in_=w_raw[:].rearrange("p j m -> p m j"))
+        nc.vector.quantize_mx(out=w_codes[:].bitcast(FP8X4), scales=w_plane[:], in_=w_bf[:].rearrange("p m j -> p (m j)"))
+
+        y = keep.tile([P, S], F32, name="y", align_bytes=64)
+        picked_all = shared.tile([P, S], U32, name="picked_all", align_bytes=64, offset=T - 64)
+        for h in range(2):
+            picked = picked_all[:, h * HALF : (h + 1) * HALF]
+            list_cols = slice(h * HALF // LIST_ROWS, (h + 1) * HALF // LIST_ROWS)
+            nc.vector.tensor_copy(picked, words[:].bitcast(U32).indirect(offs_sb[:, list_cols]))
+            lo = 0
+            for width in PIECES[h]:
+                acc = psum.tile([P, width], F32, name="acc%d_%d" % (h, lo))
+                at = h * HALF + lo
+                nc.tensor.matmul_mx(
+                    out=acc[:],
+                    lhsT=w_codes[:].bitcast(FP8X4),
+                    lhsT_scale=w_plane[:],
+                    rhs=picked[:, lo : lo + width].bitcast(FP8X4),
+                    rhs_scale=x_plane[:, at : at + width],
+                    start=True,
+                    stop=True,
+                )
+                nc.scalar.activation(out=y[:, at : at + width], in_=acc[:], func=GELU)
+                lo += width
+
+        rest = keep.tile([P, V], F32, name="rest", align_bytes=64)
+        nc.vector.tensor_scalar(out=rest[:], in0=frac_sb[:], scalar1=-1.0, scalar2=1.0, op0=MULT, op1=ADD)
+
+        from_left = keep.tile([P, V], F32, name="from_left", align_bytes=64)
+        nc.vector.tensor_tensor(from_left[:], y[:].indirect(left_sb[:]), rest[:], MULT)
+        queues = (nc.scalar, nc.sync)
+        from_right = []
+        for h in range(2):
+            cols = slice(h * OUT_PIECE, (h + 1) * OUT_PIECE)
+            list_cols = slice(h * OUT_PIECE // LIST_ROWS, (h + 1) * OUT_PIECE // LIST_ROWS)
+            part = keep.tile([P, OUT_PIECE], F32, name="from_right%d" % h, align_bytes=64)
+            nc.vector.tensor_tensor(part[:], y[:].indirect(right_sb[:, list_cols]), frac_sb[:, cols], MULT)
+            from_right.append(part)
+        for h in range(2):
+            cols = slice(h * OUT_PIECE, (h + 1) * OUT_PIECE)
+            res = keep.tile([P, OUT_PIECE], F32, name="res%d" % h, align_bytes=64)
+            nc.vector.tensor_tensor(res[:], from_left[:, cols], from_right[h][:], ADD)
+            queues[h].dma_start(out=out[:, cols], in_=res[:])

@@ -22,6 +22,7 @@ LIST_ROWS = 16
 HALF = S // 2
 PIECES = ((512,), (128, 128, 128, 128))
 OUT_PIECE = V // 2
+CLEAR_SPLIT = 2816
 
 
 def tile_picked_lerp_gelu_p_kernel(tc, x_words, x_scales, w1, frac, offs, left, right, out):
@@ -41,23 +42,21 @@ def tile_picked_lerp_gelu_p_kernel(tc, x_words, x_scales, w1, frac, offs, left, 
         x_plane = keep.tile([P, S], U8, name="x_plane", align_bytes=64)
 
         words_hbm = x_words[0].rearrange("p n t -> p (n t)").bitcast(I32)
-        for h in range(2):
-            cols = slice(h * T // 2, (h + 1) * T // 2)
-            nc.scalar.dma_start(out=words[:, cols], in_=words_hbm[:, cols])
-        nc.scalar.dma_start(out=frac_sb[:], in_=frac)
-
-        nc.vector.memset(spread[:].bitcast(I32), 0)
+        nc.vector.memset(spread[:, :CLEAR_SPLIT].bitcast(I32), 0)
+        nc.gpsimd.memset(spread[:, CLEAR_SPLIT:].bitcast(I32), 0)
         nc.gpsimd.memset(x_plane[:].bitcast(I32), 0)
+        nc.sync.dma_start(out=w_raw[:], in_=w1.rearrange("(p j) m -> p j m", j=PACK))
         nc.sync.dma_start(offs_sb[:], offs)
         nc.sync.dma_start(out=spread[4:P:8, :].bitcast(I32), in_=x_scales[0].bitcast(I32))
-        nc.sync.dma_start(out=w_raw[:], in_=w1.rearrange("(p j) m -> p j m", j=PACK))
+        nc.sync.dma_start(out=words[:], in_=words_hbm)
         nc.sync.dma_start(left_sb[:], left)
         nc.sync.dma_start(right_sb[:], right)
+        nc.sync.dma_start(out=frac_sb[:], in_=frac)
 
         picked_spread = keep.tile([P, S], U8, name="picked_spread", align_bytes=64)
         nc.vector.tensor_copy(picked_spread[:], spread[:].indirect(offs_sb[:]))
         for q in range(4):
-            nc.sync.dma_start(
+            nc.scalar.dma_start(
                 out=x_plane[32 * q : 32 * q + 4, :].bitcast(I32),
                 in_=picked_spread[32 * q + 4 : 32 * q + 32 : 8, :].bitcast(I32),
             )

@@ -1,6 +1,7 @@
 from contextlib import ExitStack
 
 import concourse.mybir as mybir
+from concourse.masks import make_identity
 
 K, T, S, V, M = 512, 4096, 1024, 512, 128
 FLOPS = 2 * K * M * S
@@ -22,7 +23,8 @@ LIST_ROWS = 16
 HALF = S // 2
 PIECES = ((512,), (128, 128, 128, 128))
 OUT_PIECE = V // 2
-CLEAR_SPLIT = 2816
+ROW0 = P - K // 32
+FRAC_COLS = V // P
 
 
 def tile_picked_lerp_gelu_p_kernel(tc, x_words, x_scales, w1, frac, offs, left, right, out):
@@ -38,27 +40,26 @@ def tile_picked_lerp_gelu_p_kernel(tc, x_words, x_scales, w1, frac, offs, left, 
         words = keep.tile([P, T], I32, name="words", align_bytes=64)
         spread = shared.tile([P, T], U8, name="spread", align_bytes=64, offset=0)
         w_raw = keep.tile([P, PACK, M], F32, name="w_raw", align_bytes=64)
-        frac_sb = keep.tile([P, V], F32, name="frac_sb", align_bytes=64)
         x_plane = keep.tile([P, S], U8, name="x_plane", align_bytes=64)
 
         words_hbm = x_words[0].rearrange("p n t -> p (n t)").bitcast(I32)
-        nc.vector.memset(spread[:, :CLEAR_SPLIT].bitcast(I32), 0)
-        nc.gpsimd.memset(spread[:, CLEAR_SPLIT:].bitcast(I32), 0)
-        nc.gpsimd.memset(x_plane[:].bitcast(I32), 0)
-        nc.sync.dma_start(out=w_raw[:], in_=w1.rearrange("(p j) m -> p j m", j=PACK))
+        nc.vector.memset(spread[:ROW0, :].bitcast(I32), 0)
+        nc.vector.memset(x_plane[:].bitcast(I32), 0)
+        nc.scalar.dma_start(out=spread[ROW0:, :].bitcast(I32), in_=x_scales[0].bitcast(I32))
         nc.sync.dma_start(offs_sb[:], offs)
-        nc.sync.dma_start(out=spread[4:P:8, :].bitcast(I32), in_=x_scales[0].bitcast(I32))
-        nc.sync.dma_start(out=words[:], in_=words_hbm)
+        nc.scalar.dma_start(out=w_raw[:], in_=w1.rearrange("(p j) m -> p j m", j=PACK))
+        nc.scalar.dma_start(out=words[:], in_=words_hbm)
+        frac_col = keep.tile([P, FRAC_COLS], F32, name="frac_col")
+        nc.sync.dma_start(out=frac_col[:], in_=frac[0].rearrange("(p t) -> p t", t=FRAC_COLS))
         nc.sync.dma_start(left_sb[:], left)
         nc.sync.dma_start(right_sb[:], right)
-        nc.sync.dma_start(out=frac_sb[:], in_=frac)
 
         picked_spread = keep.tile([P, S], U8, name="picked_spread", align_bytes=64)
         nc.vector.tensor_copy(picked_spread[:], spread[:].indirect(offs_sb[:]))
         for q in range(4):
-            nc.scalar.dma_start(
+            nc.sync.dma_start(
                 out=x_plane[32 * q : 32 * q + 4, :].bitcast(I32),
-                in_=picked_spread[32 * q + 4 : 32 * q + 32 : 8, :].bitcast(I32),
+                in_=picked_spread[ROW0 + 4 * q : ROW0 + 4 * q + 4, :].bitcast(I32),
             )
 
         w_bf = shared.tile([P, M, PACK], BF16, name="w_bf", align_bytes=64, offset=T)
@@ -66,6 +67,16 @@ def tile_picked_lerp_gelu_p_kernel(tc, x_words, x_scales, w1, frac, offs, left, 
         w_plane = keep.tile([P, M], U8, name="w_plane", align_bytes=64)
         nc.vector.tensor_copy(out=w_bf[:], in_=w_raw[:].rearrange("p j m -> p m j"))
         nc.vector.quantize_mx(out=w_codes[:].bitcast(FP8X4), scales=w_plane[:], in_=w_bf[:].rearrange("p m j -> p (m j)"))
+
+        ident = keep.tile([P, P], F32, name="ident", align_bytes=64)
+        make_identity(nc, ident[:])
+        frac_ps = psum.tile([P, FRAC_COLS, P], F32, name="frac_ps")
+        for t in range(FRAC_COLS):
+            nc.tensor.transpose(frac_ps[:, t, :], frac_col[:, t : t + 1].to_broadcast([P, P]), ident[:])
+        frac_sb = keep.tile([P, V], F32, name="frac_sb", align_bytes=64)
+        nc.vector.tensor_copy(out=frac_sb[:].rearrange("m (p t) -> m p t", t=FRAC_COLS), in_=frac_ps[:].rearrange("m t p -> m p t"))
+        rest = keep.tile([P, V], F32, name="rest", align_bytes=64)
+        nc.vector.tensor_scalar(out=rest[:], in0=frac_sb[:], scalar1=-1.0, scalar2=1.0, op0=MULT, op1=ADD)
 
         y = keep.tile([P, S], F32, name="y", align_bytes=64)
         picked_all = shared.tile([P, S], U32, name="picked_all", align_bytes=64, offset=T - 64)
@@ -88,9 +99,6 @@ def tile_picked_lerp_gelu_p_kernel(tc, x_words, x_scales, w1, frac, offs, left, 
                 )
                 nc.scalar.activation(out=y[:, at : at + width], in_=acc[:], func=GELU)
                 lo += width
-
-        rest = keep.tile([P, V], F32, name="rest", align_bytes=64)
-        nc.vector.tensor_scalar(out=rest[:], in0=frac_sb[:], scalar1=-1.0, scalar2=1.0, op0=MULT, op1=ADD)
 
         from_left = keep.tile([P, V], F32, name="from_left", align_bytes=64)
         nc.vector.tensor_tensor(from_left[:], y[:].indirect(left_sb[:]), rest[:], MULT)

@@ -21,7 +21,7 @@ P = 128
 PACK = 4
 LIST_ROWS = 16
 HALF = S // 2
-PIECES = ((512,), (128, 128, 128, 128))
+PIECES = ((256, 256), (128, 128, 128, 128))
 OUT_PIECE = V // 2
 ROW0 = P - K // 32
 FRAC_COLS = V // P
@@ -48,11 +48,12 @@ def tile_picked_lerp_gelu_p_kernel(tc, x_words, x_scales, w1, frac, offs, left, 
         nc.scalar.dma_start(out=spread[ROW0:, :].bitcast(I32), in_=x_scales[0].bitcast(I32))
         nc.sync.dma_start(offs_sb[:], offs)
         nc.scalar.dma_start(out=w_raw[:], in_=w1.rearrange("(p j) m -> p j m", j=PACK))
-        nc.scalar.dma_start(out=words[:], in_=words_hbm)
+        nc.scalar.dma_start(out=words[:, : T // 2], in_=words_hbm[:, : T // 2])
         frac_col = keep.tile([P, FRAC_COLS], F32, name="frac_col")
         nc.sync.dma_start(out=frac_col[:], in_=frac[0].rearrange("(p t) -> p t", t=FRAC_COLS))
         nc.sync.dma_start(left_sb[:], left)
         nc.sync.dma_start(right_sb[:], right)
+        nc.sync.dma_start(out=words[:, T // 2 :], in_=words_hbm[:, T // 2 :])
 
         picked_spread = keep.tile([P, S], U8, name="picked_spread", align_bytes=64)
         nc.vector.tensor_copy(picked_spread[:], spread[:].indirect(offs_sb[:]))

@@ -19,12 +19,21 @@ GELU = mybir.ActivationFunctionType.Gelu_apprx_tanh
 
 P = 128
 PACK = 4
-LIST_ROWS = 16
+BLOCK = 32
+QUADRANT = 32
+ROWS_PER_QUADRANT = 4
+PER_COLUMN = 16
+ALIGN = 64
+SCALE_ROW0 = P - K // BLOCK
+FRAC_COLS = V // P
+
 HALF = S // 2
 PIECES = ((256, 256), (128, 128, 128, 128))
 OUT_PIECE = V // 2
-ROW0 = P - K // 32
-FRAC_COLS = V // P
+
+
+def list_columns(first, count):
+    return slice(first // PER_COLUMN, (first + count) // PER_COLUMN)
 
 
 def tile_picked_lerp_gelu_p_kernel(tc, x_words, x_scales, w1, frac, offs, left, right, out):
@@ -34,85 +43,86 @@ def tile_picked_lerp_gelu_p_kernel(tc, x_words, x_scales, w1, frac, offs, left, 
         shared = ctx.enter_context(tc.tile_pool(name="shared", bufs=1))
         psum = ctx.enter_context(tc.psum_pool(name="psum", bufs=1))
 
-        offs_sb = keep.tile([P, S // LIST_ROWS], U16, name="offs_sb")
-        left_sb = keep.tile([P, V // LIST_ROWS], U16, name="left_sb")
-        right_sb = keep.tile([P, V // LIST_ROWS], U16, name="right_sb")
-        words = keep.tile([P, T], I32, name="words", align_bytes=64)
-        spread = shared.tile([P, T], U8, name="spread", align_bytes=64, offset=0)
-        w_raw = keep.tile([P, PACK, M], F32, name="w_raw", align_bytes=64)
-        x_plane = keep.tile([P, S], U8, name="x_plane", align_bytes=64)
+        offs_sb = keep.tile([P, S // PER_COLUMN], U16, name="offs_sb")
+        left_sb = keep.tile([P, V // PER_COLUMN], U16, name="left_sb")
+        right_sb = keep.tile([P, V // PER_COLUMN], U16, name="right_sb")
+        words = keep.tile([P, T], I32, name="words", align_bytes=ALIGN)
+        scale_table = shared.tile([P, T], U8, name="scale_table", align_bytes=ALIGN, offset=0)
+        w_raw = keep.tile([P, PACK, M], F32, name="w_raw", align_bytes=ALIGN)
+        x_plane = keep.tile([P, S], U8, name="x_plane", align_bytes=ALIGN)
 
         words_hbm = x_words[0].rearrange("p n t -> p (n t)").bitcast(I32)
-        nc.vector.memset(spread[:ROW0, :].bitcast(I32), 0)
+        nc.vector.memset(scale_table[:SCALE_ROW0, :].bitcast(I32), 0)
         nc.vector.memset(x_plane[:].bitcast(I32), 0)
-        nc.scalar.dma_start(out=spread[ROW0:, :].bitcast(I32), in_=x_scales[0].bitcast(I32))
+
+        nc.scalar.dma_start(out=scale_table[SCALE_ROW0:, :].bitcast(I32), in_=x_scales[0].bitcast(I32))
         nc.sync.dma_start(offs_sb[:], offs)
         nc.scalar.dma_start(out=w_raw[:], in_=w1.rearrange("(p j) m -> p j m", j=PACK))
         nc.scalar.dma_start(out=words[:, : T // 2], in_=words_hbm[:, : T // 2])
         frac_col = keep.tile([P, FRAC_COLS], F32, name="frac_col")
         nc.sync.dma_start(out=frac_col[:], in_=frac[0].rearrange("(p t) -> p t", t=FRAC_COLS))
+        nc.sync.dma_start(out=words[:, T // 2 :], in_=words_hbm[:, T // 2 :])
         nc.sync.dma_start(left_sb[:], left)
         nc.sync.dma_start(right_sb[:], right)
-        nc.sync.dma_start(out=words[:, T // 2 :], in_=words_hbm[:, T // 2 :])
 
-        picked_spread = keep.tile([P, S], U8, name="picked_spread", align_bytes=64)
-        nc.vector.tensor_copy(picked_spread[:], spread[:].indirect(offs_sb[:]))
-        for q in range(4):
+        picked_scales = keep.tile([P, S], U8, name="picked_scales", align_bytes=ALIGN)
+        nc.vector.tensor_copy(picked_scales[:], scale_table[:].indirect(offs_sb[:]))
+        for q in range(P // QUADRANT):
+            src_row = SCALE_ROW0 + ROWS_PER_QUADRANT * q
             nc.sync.dma_start(
-                out=x_plane[32 * q : 32 * q + 4, :].bitcast(I32),
-                in_=picked_spread[ROW0 + 4 * q : ROW0 + 4 * q + 4, :].bitcast(I32),
+                out=x_plane[QUADRANT * q : QUADRANT * q + ROWS_PER_QUADRANT, :].bitcast(I32),
+                in_=picked_scales[src_row : src_row + ROWS_PER_QUADRANT, :].bitcast(I32),
             )
 
-        w_bf = shared.tile([P, M, PACK], BF16, name="w_bf", align_bytes=64, offset=T)
-        w_codes = keep.tile([P, M], U32, name="w_codes", align_bytes=64)
-        w_plane = keep.tile([P, M], U8, name="w_plane", align_bytes=64)
+        w_bf = shared.tile([P, M, PACK], BF16, name="w_bf", align_bytes=ALIGN, offset=T)
+        w_codes = keep.tile([P, M], U32, name="w_codes", align_bytes=ALIGN)
+        w_plane = keep.tile([P, M], U8, name="w_plane", align_bytes=ALIGN)
         nc.vector.tensor_copy(out=w_bf[:], in_=w_raw[:].rearrange("p j m -> p m j"))
         nc.vector.quantize_mx(out=w_codes[:].bitcast(FP8X4), scales=w_plane[:], in_=w_bf[:].rearrange("p m j -> p (m j)"))
 
-        ident = keep.tile([P, P], F32, name="ident", align_bytes=64)
+        ident = keep.tile([P, P], F32, name="ident", align_bytes=ALIGN)
         make_identity(nc, ident[:])
         frac_ps = psum.tile([P, FRAC_COLS, P], F32, name="frac_ps")
         for t in range(FRAC_COLS):
             nc.tensor.transpose(frac_ps[:, t, :], frac_col[:, t : t + 1].to_broadcast([P, P]), ident[:])
-        frac_sb = keep.tile([P, V], F32, name="frac_sb", align_bytes=64)
+        frac_sb = keep.tile([P, V], F32, name="frac_sb", align_bytes=ALIGN)
         nc.vector.tensor_copy(out=frac_sb[:].rearrange("m (p t) -> m p t", t=FRAC_COLS), in_=frac_ps[:].rearrange("m t p -> m p t"))
-        rest = keep.tile([P, V], F32, name="rest", align_bytes=64)
-        nc.vector.tensor_scalar(out=rest[:], in0=frac_sb[:], scalar1=-1.0, scalar2=1.0, op0=MULT, op1=ADD)
+        one_minus_frac = keep.tile([P, V], F32, name="one_minus_frac", align_bytes=ALIGN)
+        nc.vector.tensor_scalar(out=one_minus_frac[:], in0=frac_sb[:], scalar1=-1.0, scalar2=1.0, op0=MULT, op1=ADD)
 
-        y = keep.tile([P, S], F32, name="y", align_bytes=64)
-        picked_all = shared.tile([P, S], U32, name="picked_all", align_bytes=64, offset=T - 64)
-        for h in range(2):
-            picked = picked_all[:, h * HALF : (h + 1) * HALF]
-            list_cols = slice(h * HALF // LIST_ROWS, (h + 1) * HALF // LIST_ROWS)
-            nc.vector.tensor_copy(picked, words[:].bitcast(U32).indirect(offs_sb[:, list_cols]))
-            lo = 0
-            for width in PIECES[h]:
-                acc = psum.tile([P, width], F32, name="acc%d_%d" % (h, lo))
-                at = h * HALF + lo
+        y = keep.tile([P, S], F32, name="y", align_bytes=ALIGN)
+        picked_words = shared.tile([P, S], U32, name="picked_words", align_bytes=ALIGN, offset=T - ALIGN)
+        for half, widths in enumerate(PIECES):
+            first = half * HALF
+            nc.vector.tensor_copy(
+                picked_words[:, first : first + HALF],
+                words[:].bitcast(U32).indirect(offs_sb[:, list_columns(first, HALF)]),
+            )
+            for width in widths:
+                cols = slice(first, first + width)
+                acc = psum.tile([P, width], F32, name="acc%d" % first)
                 nc.tensor.matmul_mx(
                     out=acc[:],
                     lhsT=w_codes[:].bitcast(FP8X4),
                     lhsT_scale=w_plane[:],
-                    rhs=picked[:, lo : lo + width].bitcast(FP8X4),
-                    rhs_scale=x_plane[:, at : at + width],
+                    rhs=picked_words[:, cols].bitcast(FP8X4),
+                    rhs_scale=x_plane[:, cols],
                     start=True,
                     stop=True,
                 )
-                nc.scalar.activation(out=y[:, at : at + width], in_=acc[:], func=GELU)
-                lo += width
+                nc.scalar.activation(out=y[:, cols], in_=acc[:], func=GELU)
+                first += width
 
-        from_left = keep.tile([P, V], F32, name="from_left", align_bytes=64)
-        nc.vector.tensor_tensor(from_left[:], y[:].indirect(left_sb[:]), rest[:], MULT)
-        queues = (nc.scalar, nc.sync)
+        from_left = keep.tile([P, V], F32, name="from_left", align_bytes=ALIGN)
+        nc.vector.tensor_tensor(from_left[:], y[:].indirect(left_sb[:]), one_minus_frac[:], MULT)
+        out_cols = [slice(v, v + OUT_PIECE) for v in range(0, V, OUT_PIECE)]
         from_right = []
-        for h in range(2):
-            cols = slice(h * OUT_PIECE, (h + 1) * OUT_PIECE)
-            list_cols = slice(h * OUT_PIECE // LIST_ROWS, (h + 1) * OUT_PIECE // LIST_ROWS)
-            part = keep.tile([P, OUT_PIECE], F32, name="from_right%d" % h, align_bytes=64)
-            nc.vector.tensor_tensor(part[:], y[:].indirect(right_sb[:, list_cols]), frac_sb[:, cols], MULT)
+        for cols in out_cols:
+            part = keep.tile([P, OUT_PIECE], F32, name="from_right%d" % cols.start, align_bytes=ALIGN)
+            entries = right_sb[:, list_columns(cols.start, OUT_PIECE)]
+            nc.vector.tensor_tensor(part[:], y[:].indirect(entries), frac_sb[:, cols], MULT)
             from_right.append(part)
-        for h in range(2):
-            cols = slice(h * OUT_PIECE, (h + 1) * OUT_PIECE)
-            res = keep.tile([P, OUT_PIECE], F32, name="res%d" % h, align_bytes=64)
-            nc.vector.tensor_tensor(res[:], from_left[:, cols], from_right[h][:], ADD)
-            queues[h].dma_start(out=out[:, cols], in_=res[:])
+        for cols, part, queue in zip(out_cols, from_right, (nc.scalar, nc.sync)):
+            result = keep.tile([P, OUT_PIECE], F32, name="result%d" % cols.start, align_bytes=ALIGN)
+            nc.vector.tensor_tensor(result[:], from_left[:, cols], part[:], ADD)
+            queue.dma_start(out=out[:, cols], in_=result[:])

from contextlib import ExitStack

import concourse.mybir as mybir
from concourse.masks import make_identity

K, T, S, V, M = 512, 4096, 1024, 512, 128
FLOPS = 2 * K * M * S

F32 = mybir.dt.float32
BF16 = mybir.dt.bfloat16
I32 = mybir.dt.int32
U32 = mybir.dt.uint32
U16 = mybir.dt.uint16
U8 = mybir.dt.uint8
FP8X4 = mybir.dt.float8_e4m3fn_x4
MULT = mybir.AluOpType.mult
ADD = mybir.AluOpType.add
GELU = mybir.ActivationFunctionType.Gelu_apprx_tanh

P = 128
PACK = 4
BLOCK = 32
QUADRANT = 32
ROWS_PER_QUADRANT = 4
PER_COLUMN = 16
ALIGN = 64
SCALE_ROW0 = P - K // BLOCK
FRAC_COLS = V // P

HALF = S // 2
PIECES = ((256, 256), (128, 128, 128, 128))
OUT_PIECE = V // 2


def list_columns(first, count):
    return slice(first // PER_COLUMN, (first + count) // PER_COLUMN)


def tile_picked_lerp_gelu_p_kernel(tc, x_words, x_scales, w1, frac, offs, left, right, out):
    nc = tc.nc
    with ExitStack() as ctx:
        keep = ctx.enter_context(tc.tile_pool(name="keep", bufs=1))
        shared = ctx.enter_context(tc.tile_pool(name="shared", bufs=1))
        psum = ctx.enter_context(tc.psum_pool(name="psum", bufs=1))

        offs_sb = keep.tile([P, S // PER_COLUMN], U16, name="offs_sb")
        left_sb = keep.tile([P, V // PER_COLUMN], U16, name="left_sb")
        right_sb = keep.tile([P, V // PER_COLUMN], U16, name="right_sb")
        words = keep.tile([P, T], I32, name="words", align_bytes=ALIGN)
        scale_table = shared.tile([P, T], U8, name="scale_table", align_bytes=ALIGN, offset=0)
        w_raw = keep.tile([P, PACK, M], F32, name="w_raw", align_bytes=ALIGN)
        x_plane = keep.tile([P, S], U8, name="x_plane", align_bytes=ALIGN)

        words_hbm = x_words[0].rearrange("p n t -> p (n t)").bitcast(I32)
        nc.vector.memset(scale_table[:SCALE_ROW0, :].bitcast(I32), 0)
        nc.vector.memset(x_plane[:].bitcast(I32), 0)

        nc.scalar.dma_start(out=scale_table[SCALE_ROW0:, :].bitcast(I32), in_=x_scales[0].bitcast(I32))
        nc.sync.dma_start(offs_sb[:], offs)
        nc.scalar.dma_start(out=w_raw[:], in_=w1.rearrange("(p j) m -> p j m", j=PACK))
        nc.scalar.dma_start(out=words[:, : T // 2], in_=words_hbm[:, : T // 2])
        frac_col = keep.tile([P, FRAC_COLS], F32, name="frac_col")
        nc.sync.dma_start(out=frac_col[:], in_=frac[0].rearrange("(p t) -> p t", t=FRAC_COLS))
        nc.sync.dma_start(out=words[:, T // 2 :], in_=words_hbm[:, T // 2 :])
        nc.sync.dma_start(left_sb[:], left)
        nc.sync.dma_start(right_sb[:], right)

        picked_scales = keep.tile([P, S], U8, name="picked_scales", align_bytes=ALIGN)
        nc.vector.tensor_copy(picked_scales[:], scale_table[:].indirect(offs_sb[:]))
        for q in range(P // QUADRANT):
            src_row = SCALE_ROW0 + ROWS_PER_QUADRANT * q
            nc.sync.dma_start(
                out=x_plane[QUADRANT * q : QUADRANT * q + ROWS_PER_QUADRANT, :].bitcast(I32),
                in_=picked_scales[src_row : src_row + ROWS_PER_QUADRANT, :].bitcast(I32),
            )

        w_bf = shared.tile([P, M, PACK], BF16, name="w_bf", align_bytes=ALIGN, offset=T)
        w_codes = keep.tile([P, M], U32, name="w_codes", align_bytes=ALIGN)
        w_plane = keep.tile([P, M], U8, name="w_plane", align_bytes=ALIGN)
        nc.vector.tensor_copy(out=w_bf[:], in_=w_raw[:].rearrange("p j m -> p m j"))
        nc.vector.quantize_mx(out=w_codes[:].bitcast(FP8X4), scales=w_plane[:], in_=w_bf[:].rearrange("p m j -> p (m j)"))

        ident = keep.tile([P, P], F32, name="ident", align_bytes=ALIGN)
        make_identity(nc, ident[:])
        frac_ps = psum.tile([P, FRAC_COLS, P], F32, name="frac_ps")
        for t in range(FRAC_COLS):
            nc.tensor.transpose(frac_ps[:, t, :], frac_col[:, t : t + 1].to_broadcast([P, P]), ident[:])
        frac_sb = keep.tile([P, V], F32, name="frac_sb", align_bytes=ALIGN)
        nc.vector.tensor_copy(out=frac_sb[:].rearrange("m (p t) -> m p t", t=FRAC_COLS), in_=frac_ps[:].rearrange("m t p -> m p t"))
        one_minus_frac = keep.tile([P, V], F32, name="one_minus_frac", align_bytes=ALIGN)
        nc.vector.tensor_scalar(out=one_minus_frac[:], in0=frac_sb[:], scalar1=-1.0, scalar2=1.0, op0=MULT, op1=ADD)

        y = keep.tile([P, S], F32, name="y", align_bytes=ALIGN)
        picked_words = shared.tile([P, S], U32, name="picked_words", align_bytes=ALIGN, offset=T - ALIGN)
        for half, widths in enumerate(PIECES):
            first = half * HALF
            nc.vector.tensor_copy(
                picked_words[:, first : first + HALF],
                words[:].bitcast(U32).indirect(offs_sb[:, list_columns(first, HALF)]),
            )
            for width in widths:
                cols = slice(first, first + width)
                acc = psum.tile([P, width], F32, name="acc%d" % first)
                nc.tensor.matmul_mx(
                    out=acc[:],
                    lhsT=w_codes[:].bitcast(FP8X4),
                    lhsT_scale=w_plane[:],
                    rhs=picked_words[:, cols].bitcast(FP8X4),
                    rhs_scale=x_plane[:, cols],
                    start=True,
                    stop=True,
                )
                nc.scalar.activation(out=y[:, cols], in_=acc[:], func=GELU)
                first += width

        from_left = keep.tile([P, V], F32, name="from_left", align_bytes=ALIGN)
        nc.vector.tensor_tensor(from_left[:], y[:].indirect(left_sb[:]), one_minus_frac[:], MULT)
        out_cols = [slice(v, v + OUT_PIECE) for v in range(0, V, OUT_PIECE)]
        from_right = []
        for cols in out_cols:
            part = keep.tile([P, OUT_PIECE], F32, name="from_right%d" % cols.start, align_bytes=ALIGN)
            entries = right_sb[:, list_columns(cols.start, OUT_PIECE)]
            nc.vector.tensor_tensor(part[:], y[:].indirect(entries), frac_sb[:, cols], MULT)
            from_right.append(part)
        for cols, part, queue in zip(out_cols, from_right, (nc.scalar, nc.sync)):
            result = keep.tile([P, OUT_PIECE], F32, name="result%d" % cols.start, align_bytes=ALIGN)
            nc.vector.tensor_tensor(result[:], from_left[:, cols], part[:], ADD)
            queue.dma_start(out=out[:, cols], in_=result[:])
